import numpy as np
import ml_dtypes

BF16 = ml_dtypes.bfloat16


def bf(x):
    return np.asarray(x, np.float32).astype(BF16)


def f32(x):
    return np.asarray(x, np.float32)


def f64(x):
    return np.asarray(x).astype(np.float64)


def striped(idx):
    return np.tile(idx.reshape(-1, 16).T, (8, 1))


def rows(idx, k):
    return np.tile(idx, (k, 1))


def look(tab, idx):
    return np.take_along_axis(f64(tab), rows(idx, len(tab)), axis=1)


K, S, V, N, M = 256, 2048, 1536, 1536, 256


def setup_inputs():
    return {"tab": f32(np.random.standard_normal((2, K, S))), "y": f32(np.random.standard_normal((K, V))), "w": bf(np.random.standard_normal((K, M)) / np.sqrt(K)), "b": f32(0.5 * np.random.standard_normal((M, 1))), "offs": striped(np.random.permutation(S)[:N])}


def reference(tab, y, w, b, offs):
    idx = offs[:16].T.reshape(-1)
    x = (look(tab[0], idx) - f64(y)) * (np.maximum(look(tab[1], idx), 0.0))
    return np.maximum(f64(w).T @ x + f64(b), 0.0)

@@ -1,0 +1,76 @@
+import concourse.mybir as mybir
+
+P = 128
+PIECE = 512
+FLOPS = 2 * 256 * 256 * 1536
+
+F32, BF16, U16 = mybir.dt.float32, mybir.dt.bfloat16, mybir.dt.uint16
+ALU = mybir.AluOpType
+RELU = mybir.ActivationFunctionType.Relu
+
+
+def tile_lookup_vg_subrelu_relu_kernel(tc, tab, y, w, b, offs, out):
+    nc = tc.nc
+    rows, places = tab.shape[1], tab.shape[2]
+    entries = y.shape[1]
+    row_blocks, out_blocks, pieces = rows // P, w.shape[1] // P, entries // PIECE
+
+    def block(i):
+        return slice(i * P, (i + 1) * P)
+
+    def columns(j):
+        return slice(j * PIECE, (j + 1) * PIECE)
+
+    with (
+        tc.tile_pool(name="held", bufs=1) as held,
+        tc.psum_pool(name="psum", bufs=1) as psum,
+    ):
+        offsets = held.tile([P, entries // 16], U16, name="offsets")
+        values = [held.tile([P, places], F32, name=f"values{r}") for r in range(row_blocks)]
+        gates = [held.tile([P, places], F32, name=f"gates{r}") for r in range(row_blocks)]
+        stream = [
+            [held.tile([P, PIECE], F32, name=f"stream{r}_{j}") for j in range(pieces)]
+            for r in range(row_blocks)
+        ]
+        weights = held.tile([P, row_blocks, w.shape[1]], BF16, name="weights")
+        bias = [held.tile([P, 1], F32, name=f"bias{h}") for h in range(out_blocks)]
+        sums = [
+            [psum.tile([P, PIECE], F32, name=f"sums{h}_{j}") for j in range(pieces)]
+            for h in range(out_blocks)
+        ]
+
+        nc.sync.dma_start(offsets[:], offs)
+        for r in range(row_blocks):
+            nc.sync.dma_start(gates[r][:], tab[1, block(r), :])
+            nc.sync.dma_start(values[r][:], tab[0, block(r), :])
+            for j in range(pieces):
+                nc.sync.dma_start(stream[r][j][:], y[block(r), columns(j)])
+        nc.sync.dma_start(weights[:], w.rearrange("(r p) m -> p r m", p=P))
+        for h in range(out_blocks):
+            nc.sync.dma_start(bias[h][:], b[block(h), :])
+
+        for r in range(row_blocks):
+            for j in range(pieces):
+                picks = offsets[:, j * PIECE // 16 : (j + 1) * PIECE // 16]
+                gate = held.tile([P, PIECE], F32, name=f"gate{r}_{j}")
+                nc.scalar.activation(gate[:], gates[r][:].indirect(picks), RELU)
+                diff = held.tile([P, PIECE], F32, name=f"diff{r}_{j}")
+                nc.vector.tensor_tensor(
+                    diff[:], values[r][:].indirect(picks), stream[r][j][:], ALU.subtract
+                )
+                x = held.tile([P, PIECE], BF16, name=f"x{r}_{j}")
+                nc.vector.tensor_tensor(x[:], diff[:], gate[:], ALU.mult)
+                for h in range(out_blocks):
+                    nc.tensor.matmul(
+                        sums[h][j][:],
+                        weights[:, r, block(h)],
+                        x[:],
+                        start=(r == 0),
+                        stop=(r == row_blocks - 1),
+                    )
+
+        for j in range(pieces):
+            for h in range(out_blocks):
+                result = held.tile([P, PIECE], F32, name=f"result{h}_{j}")
+                nc.scalar.activation(result[:], sums[h][j][:], RELU, bias=bias[h][:])
+                nc.sync.dma_start(out[block(h), columns(j)], result[:])

@@ -1,7 +1,8 @@
 import concourse.mybir as mybir
 
 P = 128
-PIECE = 512
+WIDE = 512
+NARROW = 256
 FLOPS = 2 * 256 * 256 * 1536
 
 F32, BF16, U16 = mybir.dt.float32, mybir.dt.bfloat16, mybir.dt.uint16
@@ -11,66 +12,82 @@ RELU = mybir.ActivationFunctionType.Relu
 
 def tile_lookup_vg_subrelu_relu_kernel(tc, tab, y, w, b, offs, out):
     nc = tc.nc
-    rows, places = tab.shape[1], tab.shape[2]
-    entries = y.shape[1]
-    row_blocks, out_blocks, pieces = rows // P, w.shape[1] // P, entries // PIECE
-
-    def block(i):
-        return slice(i * P, (i + 1) * P)
-
-    def columns(j):
-        return slice(j * PIECE, (j + 1) * PIECE)
+    places, entries = tab.shape[2], y.shape[1]
+    upper, lower = slice(0, P), slice(P, 2 * P)
+    wide_pieces = [slice(a, a + WIDE) for a in range(0, entries, WIDE)]
+    narrow_pieces = [slice(a, a + NARROW) for a in range(0, entries, NARROW)]
 
     with (
         tc.tile_pool(name="held", bufs=1) as held,
-        tc.psum_pool(name="psum", bufs=1) as psum,
+        tc.tile_pool(name="work", bufs=3) as work,
+        tc.psum_pool(name="psum", bufs=4) as psum,
     ):
         offsets = held.tile([P, entries // 16], U16, name="offsets")
-        values = [held.tile([P, places], F32, name=f"values{r}") for r in range(row_blocks)]
-        gates = [held.tile([P, places], F32, name=f"gates{r}") for r in range(row_blocks)]
-        stream = [
-            [held.tile([P, PIECE], F32, name=f"stream{r}_{j}") for j in range(pieces)]
-            for r in range(row_blocks)
-        ]
-        weights = held.tile([P, row_blocks, w.shape[1]], BF16, name="weights")
-        bias = [held.tile([P, 1], F32, name=f"bias{h}") for h in range(out_blocks)]
-        sums = [
-            [psum.tile([P, PIECE], F32, name=f"sums{h}_{j}") for j in range(pieces)]
-            for h in range(out_blocks)
-        ]
+        upper_values = held.tile([P, places], F32, name="upper_values")
+        upper_gates = held.tile([P, places], F32, name="upper_gates")
+        lower_values = held.tile([P, places], F32, name="lower_values")
+        lower_gates = held.tile([P, places], F32, name="lower_gates")
+        upper_y = held.tile([P, entries], F32, name="upper_y")
+        lower_y = held.tile([P, entries], F32, name="lower_y")
+        weights = held.tile([P, 2, 2 * P], BF16, name="weights")
+        bias = [held.tile([P, 1], F32, name=f"bias{h}") for h in range(2)]
+        upper_gate = held.tile([P, entries], F32, name="upper_gate")
+        lower_gate = held.tile([P, entries], F32, name="lower_gate")
+        upper_x = held.tile([P, entries], BF16, name="upper_x")
+        lower_x = held.tile([P, entries], BF16, name="lower_x")
+        results = [held.tile([P, entries], F32, name=f"result{h}") for h in range(2)]
 
+        for h, rows in enumerate((upper, lower)):
+            nc.scalar.dma_start(bias[h][:], b[rows, :])
+        nc.sync.dma_start(upper_gates[:], tab[1, upper, :])
         nc.sync.dma_start(offsets[:], offs)
-        for r in range(row_blocks):
-            nc.sync.dma_start(gates[r][:], tab[1, block(r), :])
-            nc.sync.dma_start(values[r][:], tab[0, block(r), :])
-            for j in range(pieces):
-                nc.sync.dma_start(stream[r][j][:], y[block(r), columns(j)])
+        nc.sync.dma_start(upper_y[:, :WIDE], y[upper, :WIDE])
+        nc.sync.dma_start(upper_values[:], tab[0, upper, :])
+        nc.sync.dma_start(upper_y[:, WIDE:], y[upper, WIDE:])
+        nc.sync.dma_start(lower_gates[:], tab[1, lower, :])
+        nc.sync.dma_start(lower_y[:, :WIDE], y[lower, :WIDE])
+        nc.sync.dma_start(lower_values[:], tab[0, lower, :])
+        nc.sync.dma_start(lower_y[:, WIDE:], y[lower, WIDE:])
         nc.sync.dma_start(weights[:], w.rearrange("(r p) m -> p r m", p=P))
-        for h in range(out_blocks):
-            nc.sync.dma_start(bias[h][:], b[block(h), :])
 
-        for r in range(row_blocks):
-            for j in range(pieces):
-                picks = offsets[:, j * PIECE // 16 : (j + 1) * PIECE // 16]
-                gate = held.tile([P, PIECE], F32, name=f"gate{r}_{j}")
-                nc.scalar.activation(gate[:], gates[r][:].indirect(picks), RELU)
-                diff = held.tile([P, PIECE], F32, name=f"diff{r}_{j}")
-                nc.vector.tensor_tensor(
-                    diff[:], values[r][:].indirect(picks), stream[r][j][:], ALU.subtract
-                )
-                x = held.tile([P, PIECE], BF16, name=f"x{r}_{j}")
-                nc.vector.tensor_tensor(x[:], diff[:], gate[:], ALU.mult)
-                for h in range(out_blocks):
+        def picks(piece):
+            return offsets[:, piece.start // 16 : piece.stop // 16]
+
+        def difference(values, stream, piece):
+            diff = work.tile([P, piece.stop - piece.start], F32, name="diff")
+            nc.vector.tensor_tensor(
+                diff[:], values[:].indirect(picks(piece)), stream[:, piece], ALU.subtract
+            )
+            return diff
+
+        def dense_layer(piece):
+            sums = [psum.tile([P, NARROW], F32, name=f"sums{h}") for h in range(2)]
+            for r, x in enumerate((upper_x, lower_x)):
+                for h, rows in enumerate((upper, lower)):
                     nc.tensor.matmul(
-                        sums[h][j][:],
-                        weights[:, r, block(h)],
-                        x[:],
-                        start=(r == 0),
-                        stop=(r == row_blocks - 1),
+                        sums[h][:], weights[:, r, rows], x[:, piece], start=(r == 0), stop=(r == 1)
                     )
+            for h, rows in enumerate((upper, lower)):
+                result = results[h][:, piece]
+                if h == 1 and piece in narrow_pieces[-2:]:
+                    nc.vector.tensor_scalar(result, sums[h][:], bias[h][:], 0.0, ALU.add, ALU.max)
+                else:
+                    nc.scalar.activation(result, sums[h][:], RELU, bias=bias[h][:])
+                nc.sync.dma_start(out[rows, piece], result)
 
-        for j in range(pieces):
-            for h in range(out_blocks):
-                result = held.tile([P, PIECE], F32, name=f"result{h}_{j}")
-                nc.scalar.activation(result[:], sums[h][j][:], RELU, bias=bias[h][:])
-                nc.sync.dma_start(out[block(h), columns(j)], result[:])
+        for gate, gates in ((upper_gate, upper_gates), (lower_gate, lower_gates)):
+            for piece in wide_pieces:
+                nc.scalar.activation(gate[:, piece], gates[:].indirect(picks(piece)), RELU)
+
+        diff = difference(upper_values, upper_y, wide_pieces[0])
+        for piece, following in zip(wide_pieces, wide_pieces[1:] + [None]):
+            ahead = difference(upper_values, upper_y, following) if following else None
+            nc.vector.tensor_tensor(upper_x[:, piece], diff[:], upper_gate[:, piece], ALU.mult)
+            diff = ahead
+
+        diff = difference(lower_values, lower_y, narrow_pieces[0])
+        for piece, following in zip(narrow_pieces, narrow_pieces[1:] + [None]):
+            ahead = difference(lower_values, lower_y, following) if following else None
+            nc.vector.tensor_tensor(lower_x[:, piece], diff[:], lower_gate[:, piece], ALU.mult)
+            dense_layer(piece)
+            diff = ahead

import concourse.mybir as mybir

P = 128
WIDE = 512
NARROW = 256
FLOPS = 2 * 256 * 256 * 1536

F32, BF16, U16 = mybir.dt.float32, mybir.dt.bfloat16, mybir.dt.uint16
ALU = mybir.AluOpType
RELU = mybir.ActivationFunctionType.Relu


def tile_lookup_vg_subrelu_relu_kernel(tc, tab, y, w, b, offs, out):
    nc = tc.nc
    places, entries = tab.shape[2], y.shape[1]
    upper, lower = slice(0, P), slice(P, 2 * P)
    wide_pieces = [slice(a, a + WIDE) for a in range(0, entries, WIDE)]
    narrow_pieces = [slice(a, a + NARROW) for a in range(0, entries, NARROW)]

    with (
        tc.tile_pool(name="held", bufs=1) as held,
        tc.tile_pool(name="work", bufs=3) as work,
        tc.psum_pool(name="psum", bufs=4) as psum,
    ):
        offsets = held.tile([P, entries // 16], U16, name="offsets")
        upper_values = held.tile([P, places], F32, name="upper_values")
        upper_gates = held.tile([P, places], F32, name="upper_gates")
        lower_values = held.tile([P, places], F32, name="lower_values")
        lower_gates = held.tile([P, places], F32, name="lower_gates")
        upper_y = held.tile([P, entries], F32, name="upper_y")
        lower_y = held.tile([P, entries], F32, name="lower_y")
        weights = held.tile([P, 2, 2 * P], BF16, name="weights")
        bias = [held.tile([P, 1], F32, name=f"bias{h}") for h in range(2)]
        upper_gate = held.tile([P, entries], F32, name="upper_gate")
        lower_gate = held.tile([P, entries], F32, name="lower_gate")
        upper_x = held.tile([P, entries], BF16, name="upper_x")
        lower_x = held.tile([P, entries], BF16, name="lower_x")
        results = [held.tile([P, entries], F32, name=f"result{h}") for h in range(2)]

        for h, rows in enumerate((upper, lower)):
            nc.scalar.dma_start(bias[h][:], b[rows, :])
        nc.sync.dma_start(upper_gates[:], tab[1, upper, :])
        nc.sync.dma_start(offsets[:], offs)
        nc.sync.dma_start(upper_y[:, :WIDE], y[upper, :WIDE])
        nc.sync.dma_start(upper_values[:], tab[0, upper, :])
        nc.sync.dma_start(upper_y[:, WIDE:], y[upper, WIDE:])
        nc.sync.dma_start(lower_gates[:], tab[1, lower, :])
        nc.sync.dma_start(lower_y[:, :WIDE], y[lower, :WIDE])
        nc.sync.dma_start(lower_values[:], tab[0, lower, :])
        nc.sync.dma_start(lower_y[:, WIDE:], y[lower, WIDE:])
        nc.sync.dma_start(weights[:], w.rearrange("(r p) m -> p r m", p=P))

        def picks(piece):
            return offsets[:, piece.start // 16 : piece.stop // 16]

        def difference(values, stream, piece):
            diff = work.tile([P, piece.stop - piece.start], F32, name="diff")
            nc.vector.tensor_tensor(
                diff[:], values[:].indirect(picks(piece)), stream[:, piece], ALU.subtract
            )
            return diff

        def dense_layer(piece):
            sums = [psum.tile([P, NARROW], F32, name=f"sums{h}") for h in range(2)]
            for r, x in enumerate((upper_x, lower_x)):
                for h, rows in enumerate((upper, lower)):
                    nc.tensor.matmul(
                        sums[h][:], weights[:, r, rows], x[:, piece], start=(r == 0), stop=(r == 1)
                    )
            for h, rows in enumerate((upper, lower)):
                result = results[h][:, piece]
                if h == 1 and piece in narrow_pieces[-2:]:
                    nc.vector.tensor_scalar(result, sums[h][:], bias[h][:], 0.0, ALU.add, ALU.max)
                else:
                    nc.scalar.activation(result, sums[h][:], RELU, bias=bias[h][:])
                nc.sync.dma_start(out[rows, piece], result)

        for gate, gates in ((upper_gate, upper_gates), (lower_gate, lower_gates)):
            for piece in wide_pieces:
                nc.scalar.activation(gate[:, piece], gates[:].indirect(picks(piece)), RELU)

        diff = difference(upper_values, upper_y, wide_pieces[0])
        for piece, following in zip(wide_pieces, wide_pieces[1:] + [None]):
            ahead = difference(upper_values, upper_y, following) if following else None
            nc.vector.tensor_tensor(upper_x[:, piece], diff[:], upper_gate[:, piece], ALU.mult)
            diff = ahead

        diff = difference(lower_values, lower_y, narrow_pieces[0])
        for piece, following in zip(narrow_pieces, narrow_pieces[1:] + [None]):
            ahead = difference(lower_values, lower_y, following) if following else None
            nc.vector.tensor_tensor(lower_x[:, piece], diff[:], lower_gate[:, piece], ALU.mult)
            dense_layer(piece)
            diff = ahead
